import numpy as np
import ml_dtypes


def mxq(x, axis, fmt="e4m3"):
    dtype, down = {"e4m3": (ml_dtypes.float8_e4m3fn, 7), "e5m2": (ml_dtypes.float8_e5m2, 14)}[fmt]
    v = np.moveaxis(np.asarray(x, np.float32).astype(ml_dtypes.bfloat16).astype(np.float64), axis, -1)
    blocks = v.reshape(v.shape[:-1] + (-1, 32))
    amax = np.abs(blocks).max(-1, keepdims=True)
    byte = np.maximum(np.where(amax > 0, np.frexp(amax)[1] - 1 + 127, 0) - down, 1)
    scale = np.exp2(byte - 127.0)
    codes = (blocks / scale).astype(np.float32).astype(dtype).astype(np.float64)
    return np.moveaxis((codes * scale).reshape(v.shape), -1, axis)


WIDE = False


def mx_kscale(k, group=512):
    if not WIDE:
        return np.ones(k)
    levels = np.array([18, -18])
    if group != 512:
        return np.exp2(np.random.permutation(np.resize(levels, k // group))).repeat(group)
    if k % 512:
        return np.exp2(np.random.permutation(np.resize(levels, k // 32))).repeat(32)
    a = np.empty((k // 512, 16))
    for p in range(k // 512):
        a[p, :8] = np.random.permutation(np.resize(levels, 8))
        for g in range(8):
            far = levels[np.abs(levels - a[p, g]) >= 10]
            a[p, g + 8] = far[np.random.randint(len(far))]
    return np.exp2(a.ravel()).repeat(32)


def f64(x):
    return np.asarray(x).astype(np.float64)


E2M1 = np.array([0.0, 0.5, 1.0, 1.5, 2.0, 3.0, 4.0, 6.0, -0.0, -0.5, -1.0, -1.5, -2.0, -3.0, -4.0, -6.0])


def pack_group(w):
    k, n = w.shape
    w = f64(np.asarray(w, np.float32).astype(ml_dtypes.bfloat16)).reshape(k // 32, 32, n)
    amax = np.abs(w).max(1)
    mant, ex = np.frexp(amax / 6.0)
    byte = np.clip(np.where(amax > 0, np.where(mant > 0.5, ex, ex - 1) + 127, 1), 1, 254)
    scaled = (w * np.exp2(127.0 - byte)[:, None, :]).reshape(k, n).astype(np.float32)
    c = np.ascontiguousarray(scaled.reshape(k // 4, 4, n).transpose(0, 2, 1)).astype(ml_dtypes.float4_e2m1fn).view(np.uint8) & 0xF
    return np.ascontiguousarray((c[..., 0::2] | (c[..., 1::2] << 4)).reshape(k // 4, 2 * n)), byte.astype(np.uint8)


def unpack_group(words, scales):
    p, n = words.shape[0], scales.shape[1]
    words = np.ascontiguousarray(words).reshape(p, n, 2)
    nib = np.empty((p, n, 4), np.uint8)
    nib[..., 0::2] = words & 0xF
    nib[..., 1::2] = words >> 4
    return E2M1[nib].transpose(0, 2, 1).reshape(4 * p, n) * np.repeat(np.exp2(scales.astype(np.float64) - 127.0), 32, axis=0)


G, D, M, N = 4, 128, 256, 512


def setup_inputs():
    n = np.random.standard_normal
    s = mx_kscale(D, 0)[:, None]
    w_ = [pack_group(w) for w in n((G, D, M)) / np.sqrt(D) / s]
    u_ = [pack_group(w) for w in n((G, D, M)) / np.sqrt(D) / s]
    return {
        "x": (n((G, D, N)) * s).astype(np.float32),
        "w_words": np.stack([w[0] for w in w_]),
        "w_scales": np.stack([w[1] for w in w_]),
        "u_words": np.stack([w[0] for w in u_]),
        "u_scales": np.stack([w[1] for w in u_]),
        "r": n((G, M, N)).astype(np.float32),
    }


def reference(x, w_words, w_scales, u_words, u_scales, r):
    xq = mxq(f64(x), 1, "e4m3")
    h = np.stack([unpack_group(w_words[g], w_scales[g]) for g in range(G)]).transpose(0, 2, 1) @ xq
    g = np.stack([unpack_group(u_words[g], u_scales[g]) for g in range(G)]).transpose(0, 2, 1) @ xq
    y = 1.0 / (1.0 + np.exp(-(h))) * g
    y = y + f64(r)
    return y

@@ -1,0 +1,129 @@
+from contextlib import ExitStack
+
+import concourse.mybir as mybir
+
+G, D, M, N = 4, 128, 256, 512
+FLOPS = 2 * 2 * G * D * M * N
+
+F32 = mybir.dt.float32
+BF16 = mybir.dt.bfloat16
+I32 = mybir.dt.int32
+U32 = mybir.dt.uint32
+U8 = mybir.dt.uint8
+FP8X4 = mybir.dt.float8_e4m3fn_x4
+FP4X4 = mybir.dt.float4_e2m1fn_x4
+ACT = mybir.ActivationFunctionType
+ALU = mybir.AluOpType
+
+P = 128
+PACK = 4
+ROWS = D // PACK
+SCALE_ROWS = D // 32
+HALVES = M // P
+TILES = HALVES * G
+RUN = 4
+QUANT_COLS = 256
+VECTOR_COLS = 288
+GPSIMD_COLS = 3 * N + N // 2
+
+
+def tile_rows_gglu_sigmoid_res_kernel(tc, x, w_words, w_scales, u_words, u_scales, r, out):
+    nc = tc.nc
+    with ExitStack() as ctx:
+        sb = ctx.enter_context(tc.tile_pool(name="sb", bufs=1))
+        ps = ctx.enter_context(tc.psum_pool(name="ps", bufs=1))
+        ctx.enter_context(tc.manual_schedule())
+
+        x_raw = sb.tile([P, PACK, N], F32, name="x_raw", align_bytes=64)
+        x_bf = sb.tile([P, N * PACK], BF16, name="x_bf", align_bytes=64)
+        x_codes = sb.tile([P, N], U32, name="x_codes", align_bytes=64)
+        x_scales = sb.tile([P, N], U8, name="x_scales", align_bytes=64)
+        w_sb = sb.tile([P, 2 * M], U8, name="w_sb", align_bytes=64)
+        u_sb = sb.tile([P, 2 * M], U8, name="u_sb", align_bytes=64)
+        wu_scales = sb.tile([P, 2 * M], U8, name="wu_scales", align_bytes=64)
+        warm = sb.tile([P, 8], F32, name="warm")
+        warm_out = sb.tile([P, 8], F32, name="warm_out")
+        r_sb = [sb.tile([P, 2, N], F32, name="r_sb%d" % i) for i in range(TILES // 2)]
+        gate = [sb.tile([P, N], F32, name="gate%d" % i) for i in range(TILES)]
+        prod = [sb.tile([P, N], F32, name="prod%d" % i) for i in range(TILES)]
+        res = [sb.tile([P, N], F32, name="res%d" % i) for i in range(TILES)]
+        z_ps = [ps.tile([P, N], F32, name="z_ps%d" % g) for g in range(G)]
+        v_ps = [ps.tile([P, N], F32, name="v_ps%d" % g) for g in range(G)]
+
+        nc.vector.memset(wu_scales[:].bitcast(I32), 0)
+        nc.gpsimd.memset(warm[:], 0.0)
+        nc.scalar.activation(out=warm_out[:], in_=warm[:], func=ACT.Sigmoid)
+
+        nc.sync.dma_start(out=x_raw[:], in_=x.rearrange("g (p j) n -> (g p) j n", j=PACK))
+        nc.sync.dma_start(out=w_sb[:].bitcast(I32), in_=w_words.rearrange("g p b -> (g p) b").bitcast(I32))
+        nc.sync.dma_start(out=u_sb[:].bitcast(I32), in_=u_words.rearrange("g p b -> (g p) b").bitcast(I32))
+        for g in range(G):
+            rows = slice(ROWS * g, ROWS * g + SCALE_ROWS)
+            nc.sync.dma_start(out=wu_scales[rows, 0:M].bitcast(I32), in_=w_scales[g].bitcast(I32))
+            nc.sync.dma_start(out=wu_scales[rows, M : 2 * M].bitcast(I32), in_=u_scales[g].bitcast(I32))
+        for i in range(TILES // 2):
+            half, g0 = divmod(2 * i, G)
+            nc.sync.dma_start(
+                out=r_sb[i][:],
+                in_=r[g0 : g0 + 2, half * P : (half + 1) * P, :].rearrange("g p n -> p g n"),
+            )
+
+        def interleave(copy, c0, c1):
+            copy(
+                out=x_bf[:, PACK * c0 : PACK * c1].rearrange("p (c i j) -> p c j i", i=RUN, j=PACK),
+                in_=x_raw[:, :, c0:c1].rearrange("p j (c i) -> p c j i", i=RUN),
+            )
+
+        def quantize(c0, c1):
+            nc.vector.quantize_mx(
+                out=x_codes[:, c0:c1].bitcast(FP8X4),
+                scales=x_scales[:, c0:c1],
+                in_=x_bf[:, PACK * c0 : PACK * c1],
+            )
+
+        interleave(nc.vector.tensor_copy, 0, QUANT_COLS)
+        interleave(nc.vector.tensor_copy, QUANT_COLS, VECTOR_COLS)
+        interleave(nc.scalar.copy, VECTOR_COLS, N)
+        quantize(0, QUANT_COLS)
+        quantize(QUANT_COLS, N)
+
+        def product(bank, words, scale0, t):
+            half, g = divmod(t, G)
+            rows = slice(ROWS * g, ROWS * (g + 1))
+            nc.tensor.matmul_mx(
+                out=bank[g][:],
+                lhsT=words[rows, 2 * P * half : 2 * P * (half + 1)].bitcast(FP4X4),
+                lhsT_scale=wu_scales[rows, scale0 + P * half : scale0 + P * (half + 1)],
+                rhs=x_codes[rows, :].bitcast(FP8X4),
+                rhs_scale=x_scales[rows, :],
+                start=True,
+                stop=True,
+            )
+
+        def add_residual(engine, t, c0, c1):
+            engine.tensor_tensor(
+                out=res[t][:, c0:c1], in0=prod[t][:, c0:c1], in1=r_sb[t // 2][:, t % 2, c0:c1], op=ALU.add
+            )
+
+        def store(t):
+            half, g = divmod(t, G)
+            nc.sync.dma_start(out=out[g, half * P : (half + 1) * P, :], in_=res[t][:])
+
+        product(z_ps, w_sb, 0, 0)
+        for t in range(TILES):
+            g = t % G
+            if t + 1 < TILES:
+                product(z_ps, w_sb, 0, t + 1)
+            product(v_ps, u_sb, M, t)
+            nc.scalar.activation(out=gate[t][:], in_=z_ps[g][:], func=ACT.Sigmoid)
+            nc.vector.tensor_tensor(out=prod[t][:], in0=v_ps[g][:], in1=gate[t][:], op=ALU.mult)
+            cols = min(N, GPSIMD_COLS - t * N)
+            if cols > 0:
+                add_residual(nc.gpsimd, t, 0, cols)
+            if cols == N:
+                store(t)
+        for t in range(TILES):
+            cols = max(0, GPSIMD_COLS - t * N)
+            if cols < N:
+                add_residual(nc.vector, t, cols, N)
+                store(t)

@@ -43,30 +43,39 @@ def tile_rows_gglu_sigmoid_res_kernel(tc, x, w_words, w_scales, u_words, u_scale
         wu_scales = sb.tile([P, 2 * M], U8, name="wu_scales", align_bytes=64)
         warm = sb.tile([P, 8], F32, name="warm")
         warm_out = sb.tile([P, 8], F32, name="warm_out")
-        r_sb = [sb.tile([P, 2, N], F32, name="r_sb%d" % i) for i in range(TILES // 2)]
+        r_sb = [sb.tile([P, G, N], F32, name="r_sb%d" % i) for i in range(HALVES)]
         gate = [sb.tile([P, N], F32, name="gate%d" % i) for i in range(TILES)]
         prod = [sb.tile([P, N], F32, name="prod%d" % i) for i in range(TILES)]
         res = [sb.tile([P, N], F32, name="res%d" % i) for i in range(TILES)]
         z_ps = [ps.tile([P, N], F32, name="z_ps%d" % g) for g in range(G)]
         v_ps = [ps.tile([P, N], F32, name="v_ps%d" % g) for g in range(G)]
 
-        nc.vector.memset(wu_scales[:].bitcast(I32), 0)
-        nc.gpsimd.memset(warm[:], 0.0)
-        nc.scalar.activation(out=warm_out[:], in_=warm[:], func=ACT.Sigmoid)
+        def load_scales(queue, g):
+            rows = slice(ROWS * g, ROWS * (g + 1))
+            for c0, src in ((0, w_scales), (M, u_scales)):
+                queue.dma_start(
+                    out=wu_scales[rows, c0 : c0 + M].bitcast(I32),
+                    in_=src[g].bitcast(I32).partition_broadcast(ROWS // SCALE_ROWS),
+                )
 
+        nc.vector.memset(warm[:], 0.0)
+        load_scales(nc.scalar, 0)
+        load_scales(nc.scalar, 1)
+        load_scales(nc.gpsimd, 2)
+        load_scales(nc.gpsimd, 3)
         nc.sync.dma_start(out=x_raw[:], in_=x.rearrange("g (p j) n -> (g p) j n", j=PACK))
         nc.sync.dma_start(out=w_sb[:].bitcast(I32), in_=w_words.rearrange("g p b -> (g p) b").bitcast(I32))
         nc.sync.dma_start(out=u_sb[:].bitcast(I32), in_=u_words.rearrange("g p b -> (g p) b").bitcast(I32))
-        for g in range(G):
-            rows = slice(ROWS * g, ROWS * g + SCALE_ROWS)
-            nc.sync.dma_start(out=wu_scales[rows, 0:M].bitcast(I32), in_=w_scales[g].bitcast(I32))
-            nc.sync.dma_start(out=wu_scales[rows, M : 2 * M].bitcast(I32), in_=u_scales[g].bitcast(I32))
-        for i in range(TILES // 2):
-            half, g0 = divmod(2 * i, G)
+
+        def load_residual(half):
             nc.sync.dma_start(
-                out=r_sb[i][:],
-                in_=r[g0 : g0 + 2, half * P : (half + 1) * P, :].rearrange("g p n -> p g n"),
+                out=r_sb[half][:],
+                in_=r[:, half * P : (half + 1) * P, :].rearrange("g p n -> p g n"),
             )
+
+        load_residual(0)
+        nc.scalar.activation(out=warm_out[:], in_=warm[:], func=ACT.Sigmoid)
+        load_residual(1)
 
         def interleave(copy, c0, c1):
             copy(
@@ -102,7 +111,7 @@ def tile_rows_gglu_sigmoid_res_kernel(tc, x, w_words, w_scales, u_words, u_scale
 
         def add_residual(engine, t, c0, c1):
             engine.tensor_tensor(
-                out=res[t][:, c0:c1], in0=prod[t][:, c0:c1], in1=r_sb[t // 2][:, t % 2, c0:c1], op=ALU.add
+                out=res[t][:, c0:c1], in0=prod[t][:, c0:c1], in1=r_sb[t // G][:, t % G, c0:c1], op=ALU.add
             )
 
         def store(t):
@@ -117,13 +126,8 @@ def tile_rows_gglu_sigmoid_res_kernel(tc, x, w_words, w_scales, u_words, u_scale
             product(v_ps, u_sb, M, t)
             nc.scalar.activation(out=gate[t][:], in_=z_ps[g][:], func=ACT.Sigmoid)
             nc.vector.tensor_tensor(out=prod[t][:], in0=v_ps[g][:], in1=gate[t][:], op=ALU.mult)
-            cols = min(N, GPSIMD_COLS - t * N)
-            if cols > 0:
-                add_residual(nc.gpsimd, t, 0, cols)
-            if cols == N:
-                store(t)
-        for t in range(TILES):
-            cols = max(0, GPSIMD_COLS - t * N)
-            if cols < N:
-                add_residual(nc.vector, t, cols, N)
-                store(t)
+            if t > 0:
+                add_residual(nc.vector, t - 1, 0, N)
+                store(t - 1)
+        add_residual(nc.vector, TILES - 1, 0, N)
+        store(TILES - 1)

@@ -24,7 +24,7 @@ TILES = HALVES * G
 RUN = 4
 QUANT_COLS = 256
 VECTOR_COLS = 288
-GPSIMD_COLS = 3 * N + N // 2
+GPSIMD_TILES = 2
 
 
 def tile_rows_gglu_sigmoid_res_kernel(tc, x, w_words, w_scales, u_words, u_scales, r, out):
@@ -125,9 +125,10 @@ def tile_rows_gglu_sigmoid_res_kernel(tc, x, w_words, w_scales, u_words, u_scale
                 product(z_ps, w_sb, 0, t + 1)
             product(v_ps, u_sb, M, t)
             nc.scalar.activation(out=gate[t][:], in_=z_ps[g][:], func=ACT.Sigmoid)
-            nc.vector.tensor_tensor(out=prod[t][:], in0=v_ps[g][:], in1=gate[t][:], op=ALU.mult)
-            if t > 0:
-                add_residual(nc.vector, t - 1, 0, N)
-                store(t - 1)
-        add_residual(nc.vector, TILES - 1, 0, N)
-        store(TILES - 1)
+            nc.vector.tensor_tensor(out=prod[t][:], in0=gate[t][:], in1=v_ps[g][:], op=ALU.mult)
+            if t < GPSIMD_TILES:
+                add_residual(nc.gpsimd, t, 0, N)
+                store(t)
+        for t in range(GPSIMD_TILES, TILES):
+            add_residual(nc.vector, t, 0, N)
+            store(t)

@@ -24,7 +24,7 @@ TILES = HALVES * G
 RUN = 4
 QUANT_COLS = 256
 VECTOR_COLS = 288
-GPSIMD_TILES = 2
+FIRST_RUN = 5
 
 
 def tile_rows_gglu_sigmoid_res_kernel(tc, x, w_words, w_scales, u_words, u_scales, r, out):
@@ -119,16 +119,18 @@ def tile_rows_gglu_sigmoid_res_kernel(tc, x, w_words, w_scales, u_words, u_scale
             nc.sync.dma_start(out=out[g, half * P : (half + 1) * P, :], in_=res[t][:])
 
         product(z_ps, w_sb, 0, 0)
-        for t in range(TILES):
-            g = t % G
-            if t + 1 < TILES:
-                product(z_ps, w_sb, 0, t + 1)
-            product(v_ps, u_sb, M, t)
-            nc.scalar.activation(out=gate[t][:], in_=z_ps[g][:], func=ACT.Sigmoid)
-            nc.vector.tensor_tensor(out=prod[t][:], in0=gate[t][:], in1=v_ps[g][:], op=ALU.mult)
-            if t < GPSIMD_TILES:
-                add_residual(nc.gpsimd, t, 0, N)
+        for run in (range(0, FIRST_RUN), range(FIRST_RUN, TILES)):
+            shared = run.start + len(run) // 2
+            for t in run:
+                g = t % G
+                if t + 1 < TILES:
+                    product(z_ps, w_sb, 0, t + 1)
+                product(v_ps, u_sb, M, t)
+                nc.scalar.activation(out=gate[t][:], in_=z_ps[g][:], func=ACT.Sigmoid)
+                nc.vector.tensor_tensor(out=prod[t][:], in0=gate[t][:], in1=v_ps[g][:], op=ALU.mult)
+                if t < shared:
+                    add_residual(nc.gpsimd, t, 0, N)
+                    store(t)
+            for t in range(shared, run.stop):
+                add_residual(nc.vector, t, 0, N)
                 store(t)
-        for t in range(GPSIMD_TILES, TILES):
-            add_residual(nc.vector, t, 0, N)
-            store(t)

from contextlib import ExitStack

import concourse.mybir as mybir

G, D, M, N = 4, 128, 256, 512
FLOPS = 2 * 2 * G * D * M * N

F32 = mybir.dt.float32
BF16 = mybir.dt.bfloat16
I32 = mybir.dt.int32
U32 = mybir.dt.uint32
U8 = mybir.dt.uint8
FP8X4 = mybir.dt.float8_e4m3fn_x4
FP4X4 = mybir.dt.float4_e2m1fn_x4
ACT = mybir.ActivationFunctionType
ALU = mybir.AluOpType

P = 128
PACK = 4
ROWS = D // PACK
SCALE_ROWS = D // 32
HALVES = M // P
TILES = HALVES * G
RUN = 4
QUANT_COLS = 256
VECTOR_COLS = 288
FIRST_RUN = 5


def tile_rows_gglu_sigmoid_res_kernel(tc, x, w_words, w_scales, u_words, u_scales, r, out):
    nc = tc.nc
    with ExitStack() as ctx:
        sb = ctx.enter_context(tc.tile_pool(name="sb", bufs=1))
        ps = ctx.enter_context(tc.psum_pool(name="ps", bufs=1))
        ctx.enter_context(tc.manual_schedule())

        x_raw = sb.tile([P, PACK, N], F32, name="x_raw", align_bytes=64)
        x_bf = sb.tile([P, N * PACK], BF16, name="x_bf", align_bytes=64)
        x_codes = sb.tile([P, N], U32, name="x_codes", align_bytes=64)
        x_scales = sb.tile([P, N], U8, name="x_scales", align_bytes=64)
        w_sb = sb.tile([P, 2 * M], U8, name="w_sb", align_bytes=64)
        u_sb = sb.tile([P, 2 * M], U8, name="u_sb", align_bytes=64)
        wu_scales = sb.tile([P, 2 * M], U8, name="wu_scales", align_bytes=64)
        warm = sb.tile([P, 8], F32, name="warm")
        warm_out = sb.tile([P, 8], F32, name="warm_out")
        r_sb = [sb.tile([P, G, N], F32, name="r_sb%d" % i) for i in range(HALVES)]
        gate = [sb.tile([P, N], F32, name="gate%d" % i) for i in range(TILES)]
        prod = [sb.tile([P, N], F32, name="prod%d" % i) for i in range(TILES)]
        res = [sb.tile([P, N], F32, name="res%d" % i) for i in range(TILES)]
        z_ps = [ps.tile([P, N], F32, name="z_ps%d" % g) for g in range(G)]
        v_ps = [ps.tile([P, N], F32, name="v_ps%d" % g) for g in range(G)]

        def load_scales(queue, g):
            rows = slice(ROWS * g, ROWS * (g + 1))
            for c0, src in ((0, w_scales), (M, u_scales)):
                queue.dma_start(
                    out=wu_scales[rows, c0 : c0 + M].bitcast(I32),
                    in_=src[g].bitcast(I32).partition_broadcast(ROWS // SCALE_ROWS),
                )

        nc.vector.memset(warm[:], 0.0)
        load_scales(nc.scalar, 0)
        load_scales(nc.scalar, 1)
        load_scales(nc.gpsimd, 2)
        load_scales(nc.gpsimd, 3)
        nc.sync.dma_start(out=x_raw[:], in_=x.rearrange("g (p j) n -> (g p) j n", j=PACK))
        nc.sync.dma_start(out=w_sb[:].bitcast(I32), in_=w_words.rearrange("g p b -> (g p) b").bitcast(I32))
        nc.sync.dma_start(out=u_sb[:].bitcast(I32), in_=u_words.rearrange("g p b -> (g p) b").bitcast(I32))

        def load_residual(half):
            nc.sync.dma_start(
                out=r_sb[half][:],
                in_=r[:, half * P : (half + 1) * P, :].rearrange("g p n -> p g n"),
            )

        load_residual(0)
        nc.scalar.activation(out=warm_out[:], in_=warm[:], func=ACT.Sigmoid)
        load_residual(1)

        def interleave(copy, c0, c1):
            copy(
                out=x_bf[:, PACK * c0 : PACK * c1].rearrange("p (c i j) -> p c j i", i=RUN, j=PACK),
                in_=x_raw[:, :, c0:c1].rearrange("p j (c i) -> p c j i", i=RUN),
            )

        def quantize(c0, c1):
            nc.vector.quantize_mx(
                out=x_codes[:, c0:c1].bitcast(FP8X4),
                scales=x_scales[:, c0:c1],
                in_=x_bf[:, PACK * c0 : PACK * c1],
            )

        interleave(nc.vector.tensor_copy, 0, QUANT_COLS)
        interleave(nc.vector.tensor_copy, QUANT_COLS, VECTOR_COLS)
        interleave(nc.scalar.copy, VECTOR_COLS, N)
        quantize(0, QUANT_COLS)
        quantize(QUANT_COLS, N)

        def product(bank, words, scale0, t):
            half, g = divmod(t, G)
            rows = slice(ROWS * g, ROWS * (g + 1))
            nc.tensor.matmul_mx(
                out=bank[g][:],
                lhsT=words[rows, 2 * P * half : 2 * P * (half + 1)].bitcast(FP4X4),
                lhsT_scale=wu_scales[rows, scale0 + P * half : scale0 + P * (half + 1)],
                rhs=x_codes[rows, :].bitcast(FP8X4),
                rhs_scale=x_scales[rows, :],
                start=True,
                stop=True,
            )

        def add_residual(engine, t, c0, c1):
            engine.tensor_tensor(
                out=res[t][:, c0:c1], in0=prod[t][:, c0:c1], in1=r_sb[t // G][:, t % G, c0:c1], op=ALU.add
            )

        def store(t):
            half, g = divmod(t, G)
            nc.sync.dma_start(out=out[g, half * P : (half + 1) * P, :], in_=res[t][:])

        product(z_ps, w_sb, 0, 0)
        for run in (range(0, FIRST_RUN), range(FIRST_RUN, TILES)):
            shared = run.start + len(run) // 2
            for t in run:
                g = t % G
                if t + 1 < TILES:
                    product(z_ps, w_sb, 0, t + 1)
                product(v_ps, u_sb, M, t)
                nc.scalar.activation(out=gate[t][:], in_=z_ps[g][:], func=ACT.Sigmoid)
                nc.vector.tensor_tensor(out=prod[t][:], in0=gate[t][:], in1=v_ps[g][:], op=ALU.mult)
                if t < shared:
                    add_residual(nc.gpsimd, t, 0, N)
                    store(t)
            for t in range(shared, run.stop):
                add_residual(nc.vector, t, 0, N)
                store(t)
